import numpy as np
import ml_dtypes


def mxq(x, axis, fmt="e4m3"):
    dtype, down = {"e4m3": (ml_dtypes.float8_e4m3fn, 7), "e5m2": (ml_dtypes.float8_e5m2, 14)}[fmt]
    v = np.moveaxis(np.asarray(x, np.float32).astype(ml_dtypes.bfloat16).astype(np.float64), axis, -1)
    blocks = v.reshape(v.shape[:-1] + (-1, 32))
    amax = np.abs(blocks).max(-1, keepdims=True)
    byte = np.maximum(np.where(amax > 0, np.frexp(amax)[1] - 1 + 127, 0) - down, 1)
    scale = np.exp2(byte - 127.0)
    codes = (blocks / scale).astype(np.float32).astype(dtype).astype(np.float64)
    return np.moveaxis((codes * scale).reshape(v.shape), -1, axis)


WIDE = False


def mx_kscale(k):
    if not WIDE:
        return np.ones(k)
    levels = np.array([10, -10, 5, -5, 0])
    if k % 512:
        return np.exp2(np.random.permutation(np.resize(levels, k // 32))).repeat(32)
    a = np.empty((k // 512, 16))
    for p in range(k // 512):
        a[p, :8] = np.random.permutation(np.resize(levels, 8))
        for g in range(8):
            far = levels[np.abs(levels - a[p, g]) >= 10]
            a[p, g + 8] = far[np.random.randint(len(far))]
    return np.exp2(a.ravel()).repeat(32)


def f64(x):
    return np.asarray(x).astype(np.float64)


def striped(idx):
    return np.tile(idx.reshape(-1, 16).T, (8, 1)).astype(np.uint16)


def unstriped(offs):
    return offs[:16].T.reshape(-1).astype(np.int64)


def striped8(idx):
    return np.concatenate([x.reshape(-1, 16).T for x in idx]).astype(np.uint16)


def runs(offs, k):
    lists = np.stack([offs[16 * r : 16 * r + 16].T.reshape(-1) for r in range(8)]).astype(np.int64)
    return lists[np.arange(k) % 512 // 64]


def pack_weight(w):
    k, n = w.shape
    w = f64(np.asarray(w, np.float32).astype(ml_dtypes.bfloat16)).reshape(k // 32, 32, n)
    amax = np.abs(w).max(1)
    byte = np.clip(np.where(amax > 0, np.frexp(amax)[1] - 1 + 127 - 7, 1), 1, 254)
    scaled = (w * np.exp2(127.0 - byte)[:, None, :]).reshape(k, n).astype(np.float32)
    words = np.ascontiguousarray(scaled.reshape(k // 512, 128, 4, n).transpose(0, 1, 3, 2)).astype(ml_dtypes.float8_e4m3fn).view(np.uint8)
    return words, np.ascontiguousarray(byte.astype(np.uint8).reshape(k // 512, 16, n))


def unpack_weight(words, scales):
    g, p, n, _ = words.shape
    vals = np.ascontiguousarray(words).view(ml_dtypes.float8_e4m3fn).astype(np.float64) * np.repeat(np.exp2(scales.astype(np.float64) - 127.0), 8, axis=1)[..., None]
    return vals.transpose(0, 1, 3, 2).reshape(g * 512, n)


def gelu(v):
    return 0.5 * v * (1.0 + np.tanh(np.sqrt(2.0 / np.pi) * (v + 0.044715 * v**3)))

def planes(y):
    n, m = y.shape
    v = y.astype(np.float32).astype(ml_dtypes.bfloat16).astype(np.float64).reshape(n // 32, 32, m)
    top = np.abs(v).max(1)
    byte = np.clip(np.where(top > 0, np.frexp(top)[1] - 1 + 127 - 7, 1), 1, 254)
    codes = (v * np.exp2(127.0 - byte)[:, None, :]).reshape(n, m).astype(np.float32).astype(ml_dtypes.float8_e4m3fn).view(np.uint8)
    words = codes.reshape(n // 512, 128, 4, m).transpose(0, 1, 3, 2)
    return np.ascontiguousarray(words), np.ascontiguousarray(byte.astype(np.uint8).reshape(n // 512, 16, m))


K, T, S, G, H = 512, 2048, 512, 2048, 512


def setup_inputs():
    n = np.random.standard_normal
    s = mx_kscale(K)[:, None]
    packed_xT = pack_weight(n((K, T)) * s)
    packed_dT = pack_weight(n((K, G)) / s)
    return {
        "x_words": packed_xT[0],
        "x_scales": packed_xT[1],
        "d_words": packed_dT[0],
        "d_scales": packed_dT[1],
        "gs": (np.random.uniform(0.5, 1.5, (K, 1)) * s).astype(np.float32),
        "offs": striped(np.random.permutation(T)[:S]),
        "k1": striped8(np.random.randint(0, G, (8, H))),
        "k2": striped8(np.random.randint(0, G, (8, H))),
    }


def reference(x_words, x_scales, d_words, d_scales, gs, offs, k1, k2):
    d_k2 = unpack_weight(d_words, d_scales)[np.arange(K)[:, None], runs(k2, K)]
    d_k1 = unpack_weight(d_words, d_scales)[np.arange(K)[:, None], runs(k1, K)]
    xq = unpack_weight(x_words, x_scales)[:, unstriped(offs)]
    h = gelu(0.0625 * (d_k1.T @ xq))
    z = f64(gs) * h
    out_0 = 0.0625 * ((d_k2.T @ mxq(z, 0, "e4m3")))
    return (out_0,) + planes(out_0)

@@ -1,0 +1,154 @@
+from contextlib import ExitStack
+
+import concourse.mybir as mybir
+
+K, T, S, G, H = 512, 2048, 512, 2048, 512
+FLOPS = 2 * 2 * K * H * S
+
+F32 = mybir.dt.float32
+BF16 = mybir.dt.bfloat16
+I32 = mybir.dt.int32
+U32 = mybir.dt.uint32
+U16 = mybir.dt.uint16
+U8 = mybir.dt.uint8
+FP8X4 = mybir.dt.float8_e4m3fn_x4
+ACT = mybir.ActivationFunctionType
+
+P = 128
+PACK = 4
+CH = 128
+NCH = S // CH
+HALF = 256
+
+
+def tile_picked_pqmlp2_gelu_po_kernel(
+    tc, x_words, x_scales, d_words, d_scales, gs, offs, k1, k2, out_0, out_1, out_2
+):
+    nc = tc.nc
+    with ExitStack() as ctx:
+        keep = ctx.enter_context(tc.tile_pool(name="keep", bufs=1))
+        turn = ctx.enter_context(tc.tile_pool(name="turn", bufs=1))
+        psum = ctx.enter_context(tc.psum_pool(name="psum", bufs=1))
+
+        k1_t = keep.tile([P, H // 16], U16, name="k1_t")
+        offs_t = keep.tile([P, S // 16], U16, name="offs_t")
+        k2_t = keep.tile([P, H // 16], U16, name="k2_t")
+        gs_t = keep.tile([P, PACK], F32, name="gs_t")
+        d_win = keep.tile([P, G], I32, name="d_win", align_bytes=64)
+        x_win = turn.tile([P, T], I32, name="x_win", align_bytes=64, offset=0)
+        ds_win = keep.tile([P, G], U8, name="ds_win", align_bytes=64)
+        xs_win = keep.tile([P, T], U8, name="xs_win", align_bytes=64)
+
+        nc.vector.memset(ds_win[:].bitcast(I32), 0)
+        nc.gpsimd.memset(xs_win[:].bitcast(I32), 0)
+        placed1 = keep.tile([P, H + S], U8, name="placed1", align_bytes=64)
+        placed2 = keep.tile([P, H], U8, name="placed2", align_bytes=64)
+        nc.gpsimd.memset(placed1[:].bitcast(I32), 0)
+        nc.gpsimd.memset(placed2[:].bitcast(I32), 0)
+        nc.sync.dma_start(k1_t[:], k1)
+        nc.sync.dma_start(offs_t[:], offs)
+        nc.sync.dma_start(k2_t[:], k2)
+        nc.sync.dma_start(gs_t[:], gs.rearrange("(p t) o -> p (t o)", t=PACK))
+        for win, src in ((ds_win, d_scales), (xs_win, x_scales)):
+            nc.sync.dma_start(win[0:P:8, :].bitcast(I32), src[0].bitcast(I32))
+        nc.sync.dma_start(d_win[:], d_words[0].rearrange("p n t -> p (n t)").bitcast(I32))
+        nc.sync.dma_start(x_win[:], x_words[0].rearrange("p n t -> p (n t)").bitcast(I32))
+
+        def deal(dst, src, run):
+            nc.vector.tensor_copy(
+                out=dst.rearrange("p (t b i) -> p b t i", t=PACK, i=run),
+                in_=src.rearrange("p (b i t) -> p b t i", t=PACK, i=run),
+            )
+
+        def place_rows(queue, dst, src):
+            for r in range(4):
+                queue.dma_start(dst[r:P:32, :].bitcast(I32), src[8 * r : P : 32, :].bitcast(I32))
+
+        g1b = keep.tile([P, H + S], U8, name="g1b", align_bytes=64)
+        nc.vector.tensor_copy(g1b[:, 0:H], ds_win[:].indirect(k1_t[:]))
+        nc.vector.tensor_copy(g1b[:, H : 2 * H], ds_win[:].indirect(k2_t[:]))
+        place_rows(nc.scalar, placed1, g1b)
+        g2b = keep.tile([P, S], U8, name="g2b", align_bytes=64)
+        nc.vector.tensor_copy(g2b[:], xs_win[:].indirect(offs_t[:]))
+        place_rows(nc.scalar, placed2, g2b)
+
+        g1w = keep.tile([P, H], I32, name="g1w", align_bytes=64)
+        nc.vector.tensor_copy(g1w[:].bitcast(U32), d_win[:].bitcast(U32).indirect(k1_t[:]))
+        w1 = keep.tile([P, H], I32, name="w1", align_bytes=64)
+        deal(w1[:], g1w[:], 4)
+        plane1 = keep.tile([P, H], U8, name="plane1", align_bytes=64)
+        deal(plane1[:], placed1[:, 0:H], 16)
+        xg = []
+        for u in range(S // HALF):
+            xg.append(keep.tile([P, HALF], I32, name=f"xg{u}", align_bytes=64))
+            cols = slice(u * HALF // 16, (u + 1) * HALF // 16)
+            nc.vector.tensor_copy(xg[u][:].bitcast(U32), x_win[:].bitcast(U32).indirect(offs_t[:, cols]))
+
+        g2w = turn.tile([P, H], I32, name="g2w", align_bytes=64, offset=H)
+        nc.vector.tensor_copy(g2w[:].bitcast(U32), d_win[:].bitcast(U32).indirect(k2_t[:]))
+        w2 = keep.tile([P, H], I32, name="w2", align_bytes=64)
+        deal(w2[:], g2w[:], 4)
+        plane2 = turn.tile([P, H], U8, name="plane2", align_bytes=64, offset=0)
+        deal(plane2[:], placed1[:, H : 2 * H], 16)
+
+        def product(acc, w, w_plane, rhs, rhs_plane):
+            for t in range(PACK):
+                cols = slice(t * P, (t + 1) * P)
+                nc.tensor.matmul_mx(
+                    out=acc[:, t, :], lhsT=w[:, cols].bitcast(FP8X4), lhsT_scale=w_plane[:, cols],
+                    rhs=rhs.bitcast(FP8X4), rhs_scale=rhs_plane, start=True, stop=True,
+                )
+
+        def weave(dst, src):
+            nc.vector.tensor_copy(
+                out=dst.rearrange("p (c i) t -> p c t i", i=4),
+                in_=src.rearrange("p t (c i) -> p c t i", i=4),
+            )
+
+        groups = [(0, 2 * CH), (2 * CH, CH), (3 * CH, CH)]
+        zp = keep.tile([P, PACK, 2 * CH], BF16, name="zp", align_bytes=64)
+        hw = {}
+        for c in range(NCH):
+            acc = psum.tile([P, PACK, CH], F32, name=f"acc1_{c}")
+            u, o = divmod(c * CH, HALF)
+            product(acc, w1, plane1, xg[u][:, o : o + CH], placed2[:, c * CH : (c + 1) * CH])
+            if c < 2:
+                h = keep.tile([P, PACK, CH], F32, name=f"h{c}")
+                nc.scalar.activation(h[:], acc[:], ACT.Gelu_apprx_tanh, scale=0.0625)
+                for t in range(PACK):
+                    nc.scalar.activation(zp[:, t, c * CH : (c + 1) * CH], h[:, t, :], ACT.Copy, scale=gs_t[:, t : t + 1])
+            else:
+                hw[c * CH] = keep.tile([P, CH, PACK], F32, name=f"h{c}")
+                nc.scalar.activation(hw[c * CH][:], acc[:].rearrange("p t n -> p n t"), ACT.Gelu_apprx_tanh, scale=0.0625)
+
+        out_rows = out_0.rearrange("(p t) n -> p t n", t=PACK)
+        y_codes = keep.tile([P, S], I32, name="y_codes", align_bytes=64)
+        y_plane = keep.tile([P, S], U8, name="y_plane", align_bytes=64)
+        accs = []
+        for lo, n in groups:
+            zw = keep.tile([P, n, PACK], BF16, name=f"zw{lo}", align_bytes=64)
+            if lo == 0:
+                weave(zw[:], zp[:])
+            else:
+                nc.vector.tensor_tensor(zw[:], hw[lo][:], gs_t[:].unsqueeze(1).to_broadcast([P, n, PACK]), mybir.AluOpType.mult)
+            zc = keep.tile([P, n], I32, name=f"zc{lo}", align_bytes=64)
+            zs = keep.tile([P, n], U8, name=f"zs{lo}", align_bytes=64)
+            nc.vector.quantize_mx(out=zc[:].bitcast(FP8X4), scales=zs[:], in_=zw[:].rearrange("p n t -> p (n t)"))
+            for o in range(0, n, CH):
+                accs.append(psum.tile([P, PACK, CH], F32, name=f"acc2_{lo + o}"))
+                product(accs[-1], w2, plane2, zc[:, o : o + CH], zs[:, o : o + CH])
+        for lo, n in groups:
+            y = keep.tile([P, PACK, n], F32, name=f"y{lo}")
+            for o in range(0, n, CH):
+                nc.scalar.activation(y[:, :, o : o + CH], accs[(lo + o) // CH][:], ACT.Copy, scale=0.0625)
+            cols = slice(lo, lo + n)
+            nc.sync.dma_start(out_rows[:, :, cols], y[:])
+            yw = keep.tile([P, n, PACK], BF16, name=f"yw{lo}", align_bytes=64)
+            weave(yw[:], y[:])
+            nc.vector.quantize_mx(
+                out=y_codes[:, cols].bitcast(FP8X4), scales=y_plane[:, cols], in_=yw[:].rearrange("p n t -> p (n t)")
+            )
+        nc.sync.dma_start(out_1[0].rearrange("p n t -> p (n t)").bitcast(I32), y_codes[:])
+        for q in range(4):
+            queue = nc.scalar if q < 2 else nc.sync
+            queue.dma_start(out_2[0, 4 * q : 4 * q + 4, :].bitcast(I32), y_plane[32 * q : 32 * q + 4, :].bitcast(I32))

@@ -17,7 +17,6 @@ ACT = mybir.ActivationFunctionType
 P = 128
 PACK = 4
 CH = 128
-NCH = S // CH
 HALF = 256
 
 
@@ -35,21 +34,21 @@ def tile_picked_pqmlp2_gelu_po_kernel(
         k2_t = keep.tile([P, H // 16], U16, name="k2_t")
         gs_t = keep.tile([P, PACK], F32, name="gs_t")
         d_win = keep.tile([P, G], I32, name="d_win", align_bytes=64)
-        x_win = turn.tile([P, T], I32, name="x_win", align_bytes=64, offset=0)
+        x_win = keep.tile([P, T], I32, name="x_win", align_bytes=64)
         ds_win = keep.tile([P, G], U8, name="ds_win", align_bytes=64)
         xs_win = keep.tile([P, T], U8, name="xs_win", align_bytes=64)
-
-        nc.vector.memset(ds_win[:].bitcast(I32), 0)
-        nc.gpsimd.memset(xs_win[:].bitcast(I32), 0)
         placed1 = keep.tile([P, H + S], U8, name="placed1", align_bytes=64)
         placed2 = keep.tile([P, H], U8, name="placed2", align_bytes=64)
+
+        nc.vector.memset(xs_win[:].bitcast(I32), 0)
+        nc.gpsimd.memset(ds_win[:].bitcast(I32), 0)
         nc.gpsimd.memset(placed1[:].bitcast(I32), 0)
         nc.gpsimd.memset(placed2[:].bitcast(I32), 0)
-        nc.sync.dma_start(k1_t[:], k1)
         nc.sync.dma_start(offs_t[:], offs)
+        nc.sync.dma_start(k1_t[:], k1)
         nc.sync.dma_start(k2_t[:], k2)
         nc.sync.dma_start(gs_t[:], gs.rearrange("(p t) o -> p (t o)", t=PACK))
-        for win, src in ((ds_win, d_scales), (xs_win, x_scales)):
+        for win, src in ((xs_win, x_scales), (ds_win, d_scales)):
             nc.sync.dma_start(win[0:P:8, :].bitcast(I32), src[0].bitcast(I32))
         nc.sync.dma_start(d_win[:], d_words[0].rearrange("p n t -> p (n t)").bitcast(I32))
         nc.sync.dma_start(x_win[:], x_words[0].rearrange("p n t -> p (n t)").bitcast(I32))
@@ -64,32 +63,36 @@ def tile_picked_pqmlp2_gelu_po_kernel(
             for r in range(4):
                 queue.dma_start(dst[r:P:32, :].bitcast(I32), src[8 * r : P : 32, :].bitcast(I32))
 
-        g1b = keep.tile([P, H + S], U8, name="g1b", align_bytes=64)
+        def gather_words(dst, win, offsets):
+            nc.vector.tensor_copy(dst[:].bitcast(U32), win[:].bitcast(U32).indirect(offsets))
+
+        G1B_AT = 4 * H
+        g1b = turn.tile([P, H + S], U8, name="g1b", align_bytes=64, offset=G1B_AT)
+        nc.vector.tensor_copy(g1b[:, H : H + S], xs_win[:].indirect(offs_t[:]))
         nc.vector.tensor_copy(g1b[:, 0:H], ds_win[:].indirect(k1_t[:]))
-        nc.vector.tensor_copy(g1b[:, H : 2 * H], ds_win[:].indirect(k2_t[:]))
         place_rows(nc.scalar, placed1, g1b)
-        g2b = keep.tile([P, S], U8, name="g2b", align_bytes=64)
-        nc.vector.tensor_copy(g2b[:], xs_win[:].indirect(offs_t[:]))
+        g2b = keep.tile([P, H], U8, name="g2b", align_bytes=64)
+        nc.vector.tensor_copy(g2b[:], ds_win[:].indirect(k2_t[:]))
         place_rows(nc.scalar, placed2, g2b)
 
         g1w = keep.tile([P, H], I32, name="g1w", align_bytes=64)
-        nc.vector.tensor_copy(g1w[:].bitcast(U32), d_win[:].bitcast(U32).indirect(k1_t[:]))
+        gather_words(g1w, d_win, k1_t[:])
         w1 = keep.tile([P, H], I32, name="w1", align_bytes=64)
         deal(w1[:], g1w[:], 4)
+        xg0 = keep.tile([P, HALF], I32, name="xg0", align_bytes=64)
+        gather_words(xg0, x_win, offs_t[:, 0 : HALF // 16])
         plane1 = keep.tile([P, H], U8, name="plane1", align_bytes=64)
         deal(plane1[:], placed1[:, 0:H], 16)
-        xg = []
-        for u in range(S // HALF):
-            xg.append(keep.tile([P, HALF], I32, name=f"xg{u}", align_bytes=64))
-            cols = slice(u * HALF // 16, (u + 1) * HALF // 16)
-            nc.vector.tensor_copy(xg[u][:].bitcast(U32), x_win[:].bitcast(U32).indirect(offs_t[:, cols]))
 
-        g2w = turn.tile([P, H], I32, name="g2w", align_bytes=64, offset=H)
-        nc.vector.tensor_copy(g2w[:].bitcast(U32), d_win[:].bitcast(U32).indirect(k2_t[:]))
+        xg1 = turn.tile([P, HALF], I32, name="xg1", align_bytes=64, offset=G1B_AT + 64 + H)
+        gather_words(xg1, x_win, offs_t[:, HALF // 16 : S // 16])
+        xg = [xg0, xg1]
+        g2w = turn.tile([P, H], I32, name="g2w", align_bytes=64, offset=64)
+        gather_words(g2w, d_win, k2_t[:])
         w2 = keep.tile([P, H], I32, name="w2", align_bytes=64)
         deal(w2[:], g2w[:], 4)
-        plane2 = turn.tile([P, H], U8, name="plane2", align_bytes=64, offset=0)
-        deal(plane2[:], placed1[:, H : 2 * H], 16)
+        plane2 = turn.tile([P, H], U8, name="plane2", align_bytes=64, offset=G1B_AT + 64)
+        deal(plane2[:], placed2[:], 16)
 
         def product(acc, w, w_plane, rhs, rhs_plane):
             for t in range(PACK):
@@ -105,50 +108,55 @@ def tile_picked_pqmlp2_gelu_po_kernel(
                 in_=src.rearrange("p t (c i) -> p c t i", i=4),
             )
 
-        groups = [(0, 2 * CH), (2 * CH, CH), (3 * CH, CH)]
-        zp = keep.tile([P, PACK, 2 * CH], BF16, name="zp", align_bytes=64)
-        hw = {}
-        for c in range(NCH):
-            acc = psum.tile([P, PACK, CH], F32, name=f"acc1_{c}")
-            u, o = divmod(c * CH, HALF)
-            product(acc, w1, plane1, xg[u][:, o : o + CH], placed2[:, c * CH : (c + 1) * CH])
-            if c < 2:
-                h = keep.tile([P, PACK, CH], F32, name=f"h{c}")
-                nc.scalar.activation(h[:], acc[:], ACT.Gelu_apprx_tanh, scale=0.0625)
-                for t in range(PACK):
-                    nc.scalar.activation(zp[:, t, c * CH : (c + 1) * CH], h[:, t, :], ACT.Copy, scale=gs_t[:, t : t + 1])
-            else:
-                hw[c * CH] = keep.tile([P, CH, PACK], F32, name=f"h{c}")
-                nc.scalar.activation(hw[c * CH][:], acc[:].rearrange("p t n -> p n t"), ACT.Gelu_apprx_tanh, scale=0.0625)
+        zp, hw = [], []
+        for u in range(2):
+            acc = []
+            for o in (0, CH):
+                lo = u * HALF + o
+                acc.append(psum.tile([P, PACK, CH], F32, name=f"acc1_{lo}"))
+                product(acc[-1], w1, plane1, xg[u][:, o : o + CH], placed1[:, H + lo : H + lo + CH])
+            h = keep.tile([P, PACK, CH], F32, name=f"h{u}")
+            nc.scalar.activation(h[:], acc[0][:], ACT.Gelu_apprx_tanh, scale=0.0625)
+            hw.append(keep.tile([P, CH, PACK], F32, name=f"hw{u}"))
+            nc.scalar.activation(hw[u][:], acc[1][:].rearrange("p t n -> p n t"), ACT.Gelu_apprx_tanh, scale=0.0625)
+            zp.append(keep.tile([P, PACK, CH], BF16, name=f"zp{u}", align_bytes=64))
+            for t in range(PACK):
+                nc.scalar.activation(zp[u][:, t, :], h[:, t, :], ACT.Copy, scale=gs_t[:, t : t + 1])
 
         out_rows = out_0.rearrange("(p t) n -> p t n", t=PACK)
+        out_words = out_1[0].rearrange("p n t -> p (n t)").bitcast(I32)
         y_codes = keep.tile([P, S], I32, name="y_codes", align_bytes=64)
         y_plane = keep.tile([P, S], U8, name="y_plane", align_bytes=64)
-        accs = []
-        for lo, n in groups:
-            zw = keep.tile([P, n, PACK], BF16, name=f"zw{lo}", align_bytes=64)
-            if lo == 0:
-                weave(zw[:], zp[:])
-            else:
-                nc.vector.tensor_tensor(zw[:], hw[lo][:], gs_t[:].unsqueeze(1).to_broadcast([P, n, PACK]), mybir.AluOpType.mult)
-            zc = keep.tile([P, n], I32, name=f"zc{lo}", align_bytes=64)
-            zs = keep.tile([P, n], U8, name=f"zs{lo}", align_bytes=64)
-            nc.vector.quantize_mx(out=zc[:].bitcast(FP8X4), scales=zs[:], in_=zw[:].rearrange("p n t -> p (n t)"))
-            for o in range(0, n, CH):
-                accs.append(psum.tile([P, PACK, CH], F32, name=f"acc2_{lo + o}"))
-                product(accs[-1], w2, plane2, zc[:, o : o + CH], zs[:, o : o + CH])
-        for lo, n in groups:
-            y = keep.tile([P, PACK, n], F32, name=f"y{lo}")
-            for o in range(0, n, CH):
-                nc.scalar.activation(y[:, :, o : o + CH], accs[(lo + o) // CH][:], ACT.Copy, scale=0.0625)
-            cols = slice(lo, lo + n)
-            nc.sync.dma_start(out_rows[:, :, cols], y[:])
-            yw = keep.tile([P, n, PACK], BF16, name=f"yw{lo}", align_bytes=64)
-            weave(yw[:], y[:])
-            nc.vector.quantize_mx(
-                out=y_codes[:, cols].bitcast(FP8X4), scales=y_plane[:, cols], in_=yw[:].rearrange("p n t -> p (n t)")
-            )
-        nc.sync.dma_start(out_1[0].rearrange("p n t -> p (n t)").bitcast(I32), y_codes[:])
+        acc2 = {}
+        for u in range(2):
+            for o in (CH, 0):
+                lo = u * HALF + o
+                zw = keep.tile([P, CH, PACK], BF16, name=f"zw{lo}", align_bytes=64)
+                if o == 0:
+                    weave(zw[:], zp[u][:])
+                else:
+                    gs_b = gs_t[:].unsqueeze(1).to_broadcast([P, CH, PACK])
+                    nc.vector.tensor_tensor(zw[:], hw[u][:], gs_b, mybir.AluOpType.mult)
+                zc = keep.tile([P, CH], I32, name=f"zc{lo}", align_bytes=64)
+                zs = keep.tile([P, CH], U8, name=f"zs{lo}", align_bytes=64)
+                nc.vector.quantize_mx(out=zc[:].bitcast(FP8X4), scales=zs[:], in_=zw[:].rearrange("p n t -> p (n t)"))
+                acc2[lo] = psum.tile([P, PACK, CH], F32, name=f"acc2_{lo}")
+                product(acc2[lo], w2, plane2, zc[:], zs[:])
+        for u in range(2):
+            yw = keep.tile([P, HALF, PACK], BF16, name=f"yw{u}", align_bytes=64)
+            for o in (CH, 0):
+                lo = u * HALF + o
+                y = keep.tile([P, PACK, CH], F32, name=f"y{lo}")
+                nc.scalar.activation(y[:], acc2[lo][:], ACT.Copy, scale=0.0625)
+                nc.sync.dma_start(out_rows[:, :, lo : lo + CH], y[:])
+                weave(yw[:, o : o + CH, :], y[:])
+                cols = slice(lo, lo + CH)
+                nc.vector.quantize_mx(
+                    out=y_codes[:, cols].bitcast(FP8X4), scales=y_plane[:, cols],
+                    in_=yw[:, o : o + CH, :].rearrange("p n t -> p (n t)"),
+                )
+            cols = slice(u * HALF, (u + 1) * HALF)
+            nc.sync.dma_start(out_words[:, cols], y_codes[:, cols])
         for q in range(4):
             queue = nc.scalar if q < 2 else nc.sync
             queue.dma_start(out_2[0, 4 * q : 4 * q + 4, :].bitcast(I32), y_plane[32 * q : 32 * q + 4, :].bitcast(I32))

from contextlib import ExitStack

import concourse.mybir as mybir

K, T, S, G, H = 512, 2048, 512, 2048, 512
FLOPS = 2 * 2 * K * H * S

F32 = mybir.dt.float32
BF16 = mybir.dt.bfloat16
I32 = mybir.dt.int32
U32 = mybir.dt.uint32
U16 = mybir.dt.uint16
U8 = mybir.dt.uint8
FP8X4 = mybir.dt.float8_e4m3fn_x4
ACT = mybir.ActivationFunctionType

P = 128
PACK = 4
CH = 128
HALF = 256


def tile_picked_pqmlp2_gelu_po_kernel(
    tc, x_words, x_scales, d_words, d_scales, gs, offs, k1, k2, out_0, out_1, out_2
):
    nc = tc.nc
    with ExitStack() as ctx:
        keep = ctx.enter_context(tc.tile_pool(name="keep", bufs=1))
        turn = ctx.enter_context(tc.tile_pool(name="turn", bufs=1))
        psum = ctx.enter_context(tc.psum_pool(name="psum", bufs=1))

        k1_t = keep.tile([P, H // 16], U16, name="k1_t")
        offs_t = keep.tile([P, S // 16], U16, name="offs_t")
        k2_t = keep.tile([P, H // 16], U16, name="k2_t")
        gs_t = keep.tile([P, PACK], F32, name="gs_t")
        d_win = keep.tile([P, G], I32, name="d_win", align_bytes=64)
        x_win = keep.tile([P, T], I32, name="x_win", align_bytes=64)
        ds_win = keep.tile([P, G], U8, name="ds_win", align_bytes=64)
        xs_win = keep.tile([P, T], U8, name="xs_win", align_bytes=64)
        placed1 = keep.tile([P, H + S], U8, name="placed1", align_bytes=64)
        placed2 = keep.tile([P, H], U8, name="placed2", align_bytes=64)

        nc.vector.memset(xs_win[:].bitcast(I32), 0)
        nc.gpsimd.memset(ds_win[:].bitcast(I32), 0)
        nc.gpsimd.memset(placed1[:].bitcast(I32), 0)
        nc.gpsimd.memset(placed2[:].bitcast(I32), 0)
        nc.sync.dma_start(offs_t[:], offs)
        nc.sync.dma_start(k1_t[:], k1)
        nc.sync.dma_start(k2_t[:], k2)
        nc.sync.dma_start(gs_t[:], gs.rearrange("(p t) o -> p (t o)", t=PACK))
        for win, src in ((xs_win, x_scales), (ds_win, d_scales)):
            nc.sync.dma_start(win[0:P:8, :].bitcast(I32), src[0].bitcast(I32))
        nc.sync.dma_start(d_win[:], d_words[0].rearrange("p n t -> p (n t)").bitcast(I32))
        nc.sync.dma_start(x_win[:], x_words[0].rearrange("p n t -> p (n t)").bitcast(I32))

        def deal(dst, src, run):
            nc.vector.tensor_copy(
                out=dst.rearrange("p (t b i) -> p b t i", t=PACK, i=run),
                in_=src.rearrange("p (b i t) -> p b t i", t=PACK, i=run),
            )

        def place_rows(queue, dst, src):
            for r in range(4):
                queue.dma_start(dst[r:P:32, :].bitcast(I32), src[8 * r : P : 32, :].bitcast(I32))

        def gather_words(dst, win, offsets):
            nc.vector.tensor_copy(dst[:].bitcast(U32), win[:].bitcast(U32).indirect(offsets))

        G1B_AT = 4 * H
        g1b = turn.tile([P, H + S], U8, name="g1b", align_bytes=64, offset=G1B_AT)
        nc.vector.tensor_copy(g1b[:, H : H + S], xs_win[:].indirect(offs_t[:]))
        nc.vector.tensor_copy(g1b[:, 0:H], ds_win[:].indirect(k1_t[:]))
        place_rows(nc.scalar, placed1, g1b)
        g2b = keep.tile([P, H], U8, name="g2b", align_bytes=64)
        nc.vector.tensor_copy(g2b[:], ds_win[:].indirect(k2_t[:]))
        place_rows(nc.scalar, placed2, g2b)

        g1w = keep.tile([P, H], I32, name="g1w", align_bytes=64)
        gather_words(g1w, d_win, k1_t[:])
        w1 = keep.tile([P, H], I32, name="w1", align_bytes=64)
        deal(w1[:], g1w[:], 4)
        xg0 = keep.tile([P, HALF], I32, name="xg0", align_bytes=64)
        gather_words(xg0, x_win, offs_t[:, 0 : HALF // 16])
        plane1 = keep.tile([P, H], U8, name="plane1", align_bytes=64)
        deal(plane1[:], placed1[:, 0:H], 16)

        xg1 = turn.tile([P, HALF], I32, name="xg1", align_bytes=64, offset=G1B_AT + 64 + H)
        gather_words(xg1, x_win, offs_t[:, HALF // 16 : S // 16])
        xg = [xg0, xg1]
        g2w = turn.tile([P, H], I32, name="g2w", align_bytes=64, offset=64)
        gather_words(g2w, d_win, k2_t[:])
        w2 = keep.tile([P, H], I32, name="w2", align_bytes=64)
        deal(w2[:], g2w[:], 4)
        plane2 = turn.tile([P, H], U8, name="plane2", align_bytes=64, offset=G1B_AT + 64)
        deal(plane2[:], placed2[:], 16)

        def product(acc, w, w_plane, rhs, rhs_plane):
            for t in range(PACK):
                cols = slice(t * P, (t + 1) * P)
                nc.tensor.matmul_mx(
                    out=acc[:, t, :], lhsT=w[:, cols].bitcast(FP8X4), lhsT_scale=w_plane[:, cols],
                    rhs=rhs.bitcast(FP8X4), rhs_scale=rhs_plane, start=True, stop=True,
                )

        def weave(dst, src):
            nc.vector.tensor_copy(
                out=dst.rearrange("p (c i) t -> p c t i", i=4),
                in_=src.rearrange("p t (c i) -> p c t i", i=4),
            )

        zp, hw = [], []
        for u in range(2):
            acc = []
            for o in (0, CH):
                lo = u * HALF + o
                acc.append(psum.tile([P, PACK, CH], F32, name=f"acc1_{lo}"))
                product(acc[-1], w1, plane1, xg[u][:, o : o + CH], placed1[:, H + lo : H + lo + CH])
            h = keep.tile([P, PACK, CH], F32, name=f"h{u}")
            nc.scalar.activation(h[:], acc[0][:], ACT.Gelu_apprx_tanh, scale=0.0625)
            hw.append(keep.tile([P, CH, PACK], F32, name=f"hw{u}"))
            nc.scalar.activation(hw[u][:], acc[1][:].rearrange("p t n -> p n t"), ACT.Gelu_apprx_tanh, scale=0.0625)
            zp.append(keep.tile([P, PACK, CH], BF16, name=f"zp{u}", align_bytes=64))
            for t in range(PACK):
                nc.scalar.activation(zp[u][:, t, :], h[:, t, :], ACT.Copy, scale=gs_t[:, t : t + 1])

        out_rows = out_0.rearrange("(p t) n -> p t n", t=PACK)
        out_words = out_1[0].rearrange("p n t -> p (n t)").bitcast(I32)
        y_codes = keep.tile([P, S], I32, name="y_codes", align_bytes=64)
        y_plane = keep.tile([P, S], U8, name="y_plane", align_bytes=64)
        acc2 = {}
        for u in range(2):
            for o in (CH, 0):
                lo = u * HALF + o
                zw = keep.tile([P, CH, PACK], BF16, name=f"zw{lo}", align_bytes=64)
                if o == 0:
                    weave(zw[:], zp[u][:])
                else:
                    gs_b = gs_t[:].unsqueeze(1).to_broadcast([P, CH, PACK])
                    nc.vector.tensor_tensor(zw[:], hw[u][:], gs_b, mybir.AluOpType.mult)
                zc = keep.tile([P, CH], I32, name=f"zc{lo}", align_bytes=64)
                zs = keep.tile([P, CH], U8, name=f"zs{lo}", align_bytes=64)
                nc.vector.quantize_mx(out=zc[:].bitcast(FP8X4), scales=zs[:], in_=zw[:].rearrange("p n t -> p (n t)"))
                acc2[lo] = psum.tile([P, PACK, CH], F32, name=f"acc2_{lo}")
                product(acc2[lo], w2, plane2, zc[:], zs[:])
        for u in range(2):
            yw = keep.tile([P, HALF, PACK], BF16, name=f"yw{u}", align_bytes=64)
            for o in (CH, 0):
                lo = u * HALF + o
                y = keep.tile([P, PACK, CH], F32, name=f"y{lo}")
                nc.scalar.activation(y[:], acc2[lo][:], ACT.Copy, scale=0.0625)
                nc.sync.dma_start(out_rows[:, :, lo : lo + CH], y[:])
                weave(yw[:, o : o + CH, :], y[:])
                cols = slice(lo, lo + CH)
                nc.vector.quantize_mx(
                    out=y_codes[:, cols].bitcast(FP8X4), scales=y_plane[:, cols],
                    in_=yw[:, o : o + CH, :].rearrange("p n t -> p (n t)"),
                )
            cols = slice(u * HALF, (u + 1) * HALF)
            nc.sync.dma_start(out_words[:, cols], y_codes[:, cols])
        for q in range(4):
            queue = nc.scalar if q < 2 else nc.sync
            queue.dma_start(out_2[0, 4 * q : 4 * q + 4, :].bitcast(I32), y_plane[32 * q : 32 * q + 4, :].bitcast(I32))
